import numpy as np
import ml_dtypes


def mxq(x, axis, fmt="e4m3"):
    dtype, down = {"e4m3": (ml_dtypes.float8_e4m3fn, 7), "e5m2": (ml_dtypes.float8_e5m2, 14)}[fmt]
    v = np.moveaxis(np.asarray(x, np.float32).astype(ml_dtypes.bfloat16).astype(np.float64), axis, -1)
    blocks = v.reshape(v.shape[:-1] + (-1, 32))
    amax = np.abs(blocks).max(-1, keepdims=True)
    byte = np.maximum(np.where(amax > 0, np.frexp(amax)[1] - 1 + 127, 0) - down, 1)
    scale = np.exp2(byte - 127.0)
    codes = (blocks / scale).astype(np.float32).astype(dtype).astype(np.float64)
    return np.moveaxis((codes * scale).reshape(v.shape), -1, axis)


WIDE = False


def mx_kscale(k):
    if not WIDE:
        return np.ones(k)
    levels = np.array([24, -24, 12, -12, 0])
    if k % 512:
        return np.exp2(np.random.permutation(np.resize(levels, k // 32))).repeat(32)
    a = np.empty((k // 512, 16))
    for p in range(k // 512):
        a[p, :8] = np.random.permutation(np.resize(levels, 8))
        for g in range(8):
            far = levels[np.abs(levels - a[p, g]) >= 10]
            a[p, g + 8] = far[np.random.randint(len(far))]
    return np.exp2(a.ravel()).repeat(32)


def f64(x):
    return np.asarray(x).astype(np.float64)


def striped(idx):
    return np.tile(idx.reshape(-1, 16).T, (8, 1)).astype(np.uint16)


def unstriped(offs):
    return offs[:16].T.reshape(-1).astype(np.int64)


E2M1 = np.array([0.0, 0.5, 1.0, 1.5, 2.0, 3.0, 4.0, 6.0, -0.0, -0.5, -1.0, -1.5, -2.0, -3.0, -4.0, -6.0])


def pack_weight(w, fmt):
    k, n = w.shape
    w = f64(np.asarray(w, np.float32).astype(ml_dtypes.bfloat16)).reshape(k // 32, 32, n)
    amax = np.abs(w).max(1)
    if fmt == "e4m3":
        byte = np.frexp(amax)[1] - 1 + 127 - 7
    else:
        mant, ex = np.frexp(amax / 6.0)
        byte = np.where(mant > 0.5, ex, ex - 1) + 127
    byte = np.clip(np.where(amax > 0, byte, 1), 1, 254)
    scaled = (w * np.exp2(127.0 - byte)[:, None, :]).reshape(k, n).astype(np.float32)
    by_word = np.ascontiguousarray(scaled.reshape(k // 512, 128, 4, n).transpose(0, 1, 3, 2))
    if fmt == "e4m3":
        words = by_word.astype(ml_dtypes.float8_e4m3fn).view(np.uint8)
    else:
        c = by_word.astype(ml_dtypes.float4_e2m1fn).view(np.uint8) & 0xF
        words = (c[..., 0::2] | (c[..., 1::2] << 4)).reshape(k // 512, 128, 2 * n)
    return np.ascontiguousarray(words), np.ascontiguousarray(byte.astype(np.uint8).reshape(k // 512, 16, n))


def unpack_weight(words, scales, fmt):
    g, _, n = scales.shape
    words = np.ascontiguousarray(words).reshape(g, 128, n, -1)
    if fmt == "e4m3":
        vals = words.view(ml_dtypes.float8_e4m3fn).astype(np.float64)
    else:
        nib = np.empty((g, 128, n, 4), np.uint8)
        nib[..., 0::2] = words & 0xF
        nib[..., 1::2] = words >> 4
        vals = E2M1[nib]
    vals = vals * np.repeat(np.exp2(scales.astype(np.float64) - 127.0), 8, axis=1)[..., None]
    return vals.transpose(0, 1, 3, 2).reshape(g * 512, n)


def pack_table4(v):
    words, scales = pack_weight(v, "e2m1")
    g, t = words.shape[0] // 2, v.shape[1]
    return np.ascontiguousarray(words.reshape(g, 2, 128, t, 2).transpose(0, 2, 3, 1, 4).reshape(g, 128, t, 4)), scales


def unpack_table4(words, scales):
    g, _, t, _ = words.shape
    return unpack_weight(words.reshape(g, 128, t, 2, 2).transpose(0, 3, 1, 2, 4).reshape(2 * g, 128, 2 * t), scales, "e2m1")


K, M, N, T, J = 1024, 1024, 1024, 2048, 1024


def setup_inputs():
    n = np.random.standard_normal
    s = mx_kscale(K)[:, None]
    s2 = mx_kscale(M)[:, None]
    h = np.tanh(n((N, T)))
    p_tab = pack_table4(h * s2)
    p_wn = pack_weight(n((K, N)) / np.sqrt(K) / s, "e2m1")
    return {
        "x": (n((K, J)) * s).astype(np.float32),
        "tab_words": p_tab[0],
        "tab_scales": p_tab[1],
        "wn_words": p_wn[0],
        "wn_scales": p_wn[1],
        "un": (n((M, N)) / np.sqrt(M) / s2).astype(np.float32),
        "bn": (0.3 * n(N)).astype(np.float32),
        "hT": (h).astype(np.float32),
        "wgo": np.tile(np.random.uniform(0.5, 2.0, J), (128, 1)).astype(np.float32),
        "offs": striped(np.random.permutation(T)[:J]),
    }


def reference(x, tab_words, tab_scales, wn_words, wn_scales, un, bn, hT, wgo, offs):
    idx = unstriped(offs)
    x_ = mxq(f64(x), 0, "e4m3")
    tab_ = unpack_table4(tab_words, tab_scales)[:, idx]
    wn_ = unpack_weight(wn_words, wn_scales, "e2m1")
    un_ = mxq(f64(un), 0, "e4m3")
    sn = wn_.T @ x_ + un_.T @ tab_
    out = np.zeros((N, T))
    out[:, idx] = f64(wgo)[0] * (np.tanh(sn + f64(bn)[:, None]) + f64(hT)[:, idx])
    return out

@@ -1,0 +1,229 @@
+from contextlib import ExitStack
+
+import concourse.mybir as mybir
+from concourse.masks import make_identity
+
+K, M, N, T, J = 1024, 1024, 1024, 2048, 1024
+FLOPS = 2 * (K + M) * N * J
+
+F32 = mybir.dt.float32
+BF16 = mybir.dt.bfloat16
+I32 = mybir.dt.int32
+U32 = mybir.dt.uint32
+U16 = mybir.dt.uint16
+U8 = mybir.dt.uint8
+FP8X4 = mybir.dt.float8_e4m3fn_x4
+FP4X4 = mybir.dt.float4_e2m1fn_x4
+MULT = mybir.AluOpType.mult
+ADD = mybir.AluOpType.add
+TANH = mybir.ActivationFunctionType.Tanh
+
+P = 128
+PACK = 4
+K_PASS = P * PACK
+PASSES = K // K_PASS
+HALF = 512
+HALVES = J // HALF
+TILES = N // P
+UN_CHUNK = 256
+PAGES = 3
+SPLIT_TILES = 2
+
+
+def tile_list_tgn_rnn_kernel(
+    tc, x, tab_words, tab_scales, wn_words, wn_scales, un, bn, hT, wgo, offs, out
+):
+    nc = tc.nc
+    with ExitStack() as ctx:
+        lists = ctx.enter_context(tc.tile_pool(name="lists", bufs=1))
+        keep = ctx.enter_context(tc.tile_pool(name="keep", bufs=1))
+        ring = ctx.enter_context(tc.tile_pool(name="ring", bufs=2))
+        psum = ctx.enter_context(tc.psum_pool(name="psum", bufs=2))
+
+        def slot(tag, shape, dtype):
+            return keep.tile(shape, dtype, name="slot" + tag, tag="slot" + tag, align_bytes=64)
+
+        offsets = lists.tile([P, J // 16], U16, name="offsets")
+        nc.sync.dma_start(offsets[:], offs)
+
+        tab_s = keep.tile([P, T], U8, name="tab_s", align_bytes=64)
+        nc.sync.dma_start(tab_s[0:32, :].bitcast(I32), tab_scales.rearrange("a q t -> q a t").bitcast(I32))
+        tab_w = slot("T", [P, T], I32)
+        nc.sync.dma_start(tab_w[:], tab_words[0].rearrange("p t b -> p (t b)").bitcast(I32))
+        nc.vector.memset(tab_s[32:64, :].bitcast(I32), 0)
+        nc.vector.memset(tab_s[64:128, :].bitcast(I32), 0)
+        wn_s = keep.tile([P, PASSES, N], U8, name="wn_s", align_bytes=64)
+        v_s = keep.tile([P, PASSES, J], U8, name="v_s", align_bytes=64)
+        nc.vector.memset(wn_s[:].rearrange("p a n -> p (a n)").bitcast(I32), 0)
+        nc.vector.memset(v_s[:].rearrange("p a n -> p (a n)").bitcast(I32), 0)
+        ident = keep.tile([P, P], F32, name="ident")
+        make_identity(nc, ident[:])
+
+        v_rows = keep.tile([P, J], U8, name="v_rows", align_bytes=64)
+        nc.vector.tensor_copy(v_rows[:], tab_s[:].indirect(offsets[:]))
+        for q in range(4):
+            nc.sync.dma_start(
+                v_s[32 * q : 32 * q + 4, :, :].bitcast(I32), v_rows[8 * q : 8 * q + 8, :].bitcast(I32)
+            )
+        pages = {0: keep.tile([P, T], F32, name="page0")}
+        nc.vector.memset(pages[0][:], 0.0)
+        v_pairs = slot("C", [P, J], U32)
+        nc.vector.tensor_copy(v_pairs[:], tab_w[:].bitcast(U32).indirect(offsets[:]))
+        v_words = keep.tile([P, PASSES, J], U16, name="v_words", align_bytes=64)
+        nc.vector.tensor_copy(v_words[:], v_pairs[:].bitcast(U16).rearrange("p (j d) -> p d j", d=PASSES))
+
+        def new_page(b):
+            pages[b] = slot("P%d" % b, [P, T], F32)
+            nc.gpsimd.memset(pages[b][:], 0.0)
+
+        def load_rows(src, cols, tags):
+            width = cols.stop - cols.start
+            raws = []
+            for a in range(PASSES):
+                raw = slot(tags[a], [P, PACK, width], F32)
+                rows = src[a * K_PASS : (a + 1) * K_PASS, cols]
+                nc.sync.dma_start(raw[:], rows.rearrange("(p i) w -> p i w", i=PACK))
+                raws.append(raw)
+            return raws
+
+        def weave(copy, woven, raw):
+            copy(woven.rearrange("p (c u) i -> p c i u", u=4), raw[:].rearrange("p i (c u) -> p c i u", u=4))
+
+        def quantise(woven, codes, label):
+            scales = keep.tile([P, HALF], U8, name=label + "_scales", align_bytes=64)
+            nc.vector.quantize_mx(
+                out=codes[:].bitcast(FP8X4), scales=scales[:], in_=woven[:].rearrange("p w i -> p (w i)")
+            )
+            return codes, scales
+
+        x_q = {}
+        un_q = {}
+        h_rows = {}
+
+        def x_part(a, h, woven_tag, codes_tag):
+            woven = slot(woven_tag, [P, HALF, PACK], BF16)
+            weave(nc.scalar.copy, woven[:], x_raw[h][a])
+            x_q[a, h] = quantise(woven, slot(codes_tag, [P, HALF], U32), "x%d%d" % (a, h))
+
+        def un_weave(c, copy, woven_tag):
+            woven = slot(woven_tag, [P, PASSES * UN_CHUNK, PACK], BF16)
+            for a in range(PASSES):
+                weave(copy, woven[:, a * UN_CHUNK : (a + 1) * UN_CHUNK, :], un_raw[c][a])
+            return woven
+
+        def un_quant(c, woven, codes_tag):
+            un_q[c] = quantise(woven, slot(codes_tag, [P, PASSES * UN_CHUNK], U32), "un%d" % c)
+
+        def load_h(i, tag):
+            h_rows[i] = slot(tag, [P, T], F32)
+            nc.sync.dma_start(h_rows[i][:], hT[i * P : (i + 1) * P, :])
+
+        def update(i, h, picked, total, step_tag):
+            acc = psum.tile([P, HALF], F32, name="acc", bufs=3)
+            c, off = divmod(i * P, UN_CHUNK)
+            cols = slice(h * HALF, (h + 1) * HALF)
+            for a in range(PASSES):
+                nc.tensor.matmul_mx(
+                    out=acc[:],
+                    lhsT=wn_w[:, a, 2 * i * P : 2 * (i + 1) * P].bitcast(FP4X4),
+                    lhsT_scale=wn_s[:, a, i * P : (i + 1) * P],
+                    rhs=x_q[a, h][0][:].bitcast(FP8X4),
+                    rhs_scale=x_q[a, h][1][:],
+                    start=(a == 0),
+                    stop=False,
+                )
+            for a in range(PASSES):
+                nc.tensor.matmul_mx(
+                    out=acc[:],
+                    lhsT=un_q[c][0][:, a * UN_CHUNK + off : a * UN_CHUNK + off + P].bitcast(FP8X4),
+                    lhsT_scale=un_q[c][1][:, a * UN_CHUNK + off : a * UN_CHUNK + off + P],
+                    rhs=v_words[:, a, cols].bitcast(FP4X4),
+                    rhs_scale=v_s[:, a, cols],
+                    start=False,
+                    stop=(a == PASSES - 1),
+                )
+            if step_tag:
+                step = slot(step_tag, [P, HALF], F32)
+            else:
+                step = ring.tile([P, HALF], F32, name="step", bufs=3)
+            nc.scalar.activation(step[:], acc[:], TANH, bias=bias[:, i : i + 1])
+            if step_tag:
+                nc.vector.tensor_tensor(total, step[:], picked, ADD)
+                return
+            turned = psum.tile([P, HALF], F32, name="turned", bufs=3)
+            for b in range(HALF // P):
+                blk = slice(b * P, (b + 1) * P)
+                nc.tensor.matmul(turned[:, blk], picked[:, blk], ident[:], start=True, stop=False, is_transpose=True)
+                nc.tensor.matmul(turned[:, blk], step[:, blk], ident[:], start=False, stop=True, is_transpose=True)
+            turned_sb = ring.tile([P, HALF], F32, name="turned_sb", bufs=2)
+            nc.scalar.copy(turned_sb[:], turned[:])
+            back = psum.tile([P, HALF], F32, name="back", bufs=2)
+            for b in range(HALF // P):
+                blk = slice(b * P, (b + 1) * P)
+                nc.tensor.transpose(back[:, blk], turned_sb[:, blk], ident[:])
+            nc.scalar.copy(total, back[:])
+
+        def unit(i, halves, picked_tag, total_tag, step_tag=None):
+            width = HALF * len(halves)
+            first = halves[0] * HALF
+            entries = offsets[:, first // 16 : (first + width) // 16]
+            picked = slot(picked_tag, [P, width], F32)
+            nc.vector.tensor_copy(picked[:], h_rows[i][:].indirect(entries))
+            total = slot(total_tag, [P, width], F32)
+            for u, h in enumerate(halves):
+                part = slice(u * HALF, (u + 1) * HALF)
+                update(i, h, picked[:, part], total[:, part], step_tag)
+            page = pages[i % PAGES]
+            nc.vector.tensor_tensor(page[:].indirect(entries), total[:], gain[:, first : first + width], MULT)
+            if halves[-1] == HALVES - 1:
+                nc.sync.dma_start(out[i * P : (i + 1) * P, :], page[:])
+
+        x_raw = {}
+        un_raw = {}
+        x_raw[0] = load_rows(x, slice(0, HALF), ["R0", "R1"])
+        un_raw[0] = load_rows(un, slice(0, UN_CHUNK), ["V0", "V1"])
+        wn_w = keep.tile([P, PASSES, 2 * N], U8, name="wn_w", align_bytes=64)
+        nc.sync.dma_start(wn_w[:].bitcast(I32), wn_words.rearrange("a p b -> p a b").bitcast(I32))
+        for q in range(4):
+            nc.gpsimd.dma_start(
+                wn_s[32 * q : 32 * q + 4, :, :].bitcast(I32),
+                wn_scales[:, 4 * q : 4 * q + 4, :].rearrange("a r n -> r a n").bitcast(I32),
+            )
+        load_h(0, "H0")
+        bias = keep.tile([P, TILES], F32, name="bias")
+        with nc.allow_non_contiguous_dma(reason="one bias value a partition"):
+            nc.sync.dma_start(bias[:], bn.rearrange("(c p) -> p c", p=P))
+        gain = keep.tile([P, J], F32, name="gain")
+        nc.sync.dma_start(gain[:, 0:HALF], wgo[:, 0:HALF])
+        load_h(1, "H1")
+        x_raw[1] = load_rows(x, slice(HALF, J), ["R2", "R3"])
+        un_raw[1] = load_rows(un, slice(UN_CHUNK, 2 * UN_CHUNK), ["V2", "V3"])
+        nc.sync.dma_start(gain[:, HALF:J], wgo[:, HALF:J])
+        load_h(2, "H2")
+        load_h(3, "H3")
+
+        woven = un_weave(0, nc.vector.tensor_copy, "C")
+        x_part(0, 0, "W", "X00")
+        x_part(1, 0, "D", "X10")
+        un_quant(0, woven, "U0")
+        un_raw[2] = load_rows(un, slice(2 * UN_CHUNK, 3 * UN_CHUNK), ["V0", "V1"])
+        load_h(4, "T")
+        un_raw[3] = load_rows(un, slice(3 * UN_CHUNK, 4 * UN_CHUNK), ["R0", "R1"])
+        unit(0, [0], "D", "B", "P1")
+        new_page(1)
+        unit(1, [0], "B", "F", "P2")
+        new_page(2)
+        x_part(0, 1, "D", "F")
+        x_part(1, 1, "B", "X11")
+        un_quant(1, un_weave(1, nc.scalar.copy, "R3"), "U1")
+        unit(0, [1], "C", "G", "W")
+        load_h(5, "H0")
+        unit(1, [1], "D", "H", "S")
+        load_h(6, "H1")
+        load_h(7, "R2")
+        unit(2, [0, 1], "B", "I")
+        un_quant(2, un_weave(2, nc.scalar.copy, "B"), "H")
+        unit(3, [0, 1], "R3", "J")
+        un_quant(3, un_weave(3, nc.scalar.copy, "R3"), "I")
+        for i in range(4, TILES):
+            unit(i, [0, 1], ["B", "R3"][i % 2], "JKL"[i % 3])

@@ -46,9 +46,9 @@ def tile_list_tgn_rnn_kernel(
         offsets = lists.tile([P, J // 16], U16, name="offsets")
         nc.sync.dma_start(offsets[:], offs)
 
-        tab_s = keep.tile([P, T], U8, name="tab_s", align_bytes=64)
+        tab_s = slot("H0", [P, T], U8)
         nc.sync.dma_start(tab_s[0:32, :].bitcast(I32), tab_scales.rearrange("a q t -> q a t").bitcast(I32))
-        tab_w = slot("T", [P, T], I32)
+        tab_w = slot("H1", [P, T], I32)
         nc.sync.dma_start(tab_w[:], tab_words[0].rearrange("p t b -> p (t b)").bitcast(I32))
         nc.vector.memset(tab_s[32:64, :].bitcast(I32), 0)
         nc.vector.memset(tab_s[64:128, :].bitcast(I32), 0)
@@ -72,22 +72,28 @@ def tile_list_tgn_rnn_kernel(
         v_words = keep.tile([P, PASSES, J], U16, name="v_words", align_bytes=64)
         nc.vector.tensor_copy(v_words[:], v_pairs[:].bitcast(U16).rearrange("p (j d) -> p d j", d=PASSES))
 
-        def new_page(b):
-            pages[b] = slot("P%d" % b, [P, T], F32)
+        def new_page(b, tag):
+            pages[b] = slot(tag, [P, T], F32)
             nc.gpsimd.memset(pages[b][:], 0.0)
 
-        def load_rows(src, cols, tags):
-            width = cols.stop - cols.start
-            raws = []
+        def load_rows(raw, src, a, cols):
+            rows = src[a * K_PASS : (a + 1) * K_PASS, cols]
+            nc.sync.dma_start(raw, rows.rearrange("(p i) w -> p i w", i=PACK))
+
+        def load_x(a, h, tag):
+            raw = slot(tag, [P, PACK, HALF], F32)
+            load_rows(raw[:], x, a, slice(h * HALF, (h + 1) * HALF))
+            x_raw[a, h] = raw[:]
+
+        def load_un(c, tag):
+            raw = slot(tag, [P, PASSES * PACK * UN_CHUNK], F32)
             for a in range(PASSES):
-                raw = slot(tags[a], [P, PACK, width], F32)
-                rows = src[a * K_PASS : (a + 1) * K_PASS, cols]
-                nc.sync.dma_start(raw[:], rows.rearrange("(p i) w -> p i w", i=PACK))
-                raws.append(raw)
-            return raws
+                part = raw[:, a * PACK * UN_CHUNK : (a + 1) * PACK * UN_CHUNK].rearrange("p (i w) -> p i w", i=PACK)
+                load_rows(part, un, a, slice(c * UN_CHUNK, (c + 1) * UN_CHUNK))
+                un_raw[a, c] = part
 
         def weave(copy, woven, raw):
-            copy(woven.rearrange("p (c u) i -> p c i u", u=4), raw[:].rearrange("p i (c u) -> p c i u", u=4))
+            copy(woven.rearrange("p (c u) i -> p c i u", u=4), raw.rearrange("p i (c u) -> p c i u", u=4))
 
         def quantise(woven, codes, label):
             scales = keep.tile([P, HALF], U8, name=label + "_scales", align_bytes=64)
@@ -102,13 +108,13 @@ def tile_list_tgn_rnn_kernel(
 
         def x_part(a, h, woven_tag, codes_tag):
             woven = slot(woven_tag, [P, HALF, PACK], BF16)
-            weave(nc.scalar.copy, woven[:], x_raw[h][a])
+            weave(nc.scalar.copy, woven[:], x_raw[a, h])
             x_q[a, h] = quantise(woven, slot(codes_tag, [P, HALF], U32), "x%d%d" % (a, h))
 
         def un_weave(c, copy, woven_tag):
             woven = slot(woven_tag, [P, PASSES * UN_CHUNK, PACK], BF16)
             for a in range(PASSES):
-                weave(copy, woven[:, a * UN_CHUNK : (a + 1) * UN_CHUNK, :], un_raw[c][a])
+                weave(copy, woven[:, a * UN_CHUNK : (a + 1) * UN_CHUNK, :], un_raw[a, c])
             return woven
 
         def un_quant(c, woven, codes_tag):
@@ -118,7 +124,7 @@ def tile_list_tgn_rnn_kernel(
             h_rows[i] = slot(tag, [P, T], F32)
             nc.sync.dma_start(h_rows[i][:], hT[i * P : (i + 1) * P, :])
 
-        def update(i, h, picked, total, step_tag):
+        def activate(i, h, step_tag):
             acc = psum.tile([P, HALF], F32, name="acc", bufs=3)
             c, off = divmod(i * P, UN_CHUNK)
             cols = slice(h * HALF, (h + 1) * HALF)
@@ -147,41 +153,61 @@ def tile_list_tgn_rnn_kernel(
             else:
                 step = ring.tile([P, HALF], F32, name="step", bufs=3)
             nc.scalar.activation(step[:], acc[:], TANH, bias=bias[:, i : i + 1])
-            if step_tag:
-                nc.vector.tensor_tensor(total, step[:], picked, ADD)
-                return
+            return step
+
+        def add_turned(looked, step):
             turned = psum.tile([P, HALF], F32, name="turned", bufs=3)
             for b in range(HALF // P):
                 blk = slice(b * P, (b + 1) * P)
-                nc.tensor.matmul(turned[:, blk], picked[:, blk], ident[:], start=True, stop=False, is_transpose=True)
+                nc.tensor.matmul(turned[:, blk], looked[:, blk], ident[:], start=True, stop=False, is_transpose=True)
                 nc.tensor.matmul(turned[:, blk], step[:, blk], ident[:], start=False, stop=True, is_transpose=True)
             turned_sb = ring.tile([P, HALF], F32, name="turned_sb", bufs=2)
             nc.scalar.copy(turned_sb[:], turned[:])
+            return turned_sb
+
+        def turn_back(total, turned_sb):
             back = psum.tile([P, HALF], F32, name="back", bufs=2)
             for b in range(HALF // P):
                 blk = slice(b * P, (b + 1) * P)
                 nc.tensor.transpose(back[:, blk], turned_sb[:, blk], ident[:])
             nc.scalar.copy(total, back[:])
 
-        def unit(i, halves, picked_tag, total_tag, step_tag=None):
-            width = HALF * len(halves)
-            first = halves[0] * HALF
-            entries = offsets[:, first // 16 : (first + width) // 16]
-            picked = slot(picked_tag, [P, width], F32)
-            nc.vector.tensor_copy(picked[:], h_rows[i][:].indirect(entries))
-            total = slot(total_tag, [P, width], F32)
-            for u, h in enumerate(halves):
-                part = slice(u * HALF, (u + 1) * HALF)
-                update(i, h, picked[:, part], total[:, part], step_tag)
+        picked = {}
+        totals = {}
+
+        def entries(halves):
+            return offsets[:, halves[0] * HALF // 16 : (halves[-1] + 1) * HALF // 16]
+
+        def gather(i, halves, tag):
+            picked[i, halves[0]] = slot(tag, [P, HALF * len(halves)], F32)
+            nc.vector.tensor_copy(picked[i, halves[0]][:], h_rows[i][:].indirect(entries(halves)))
+
+        def combine(i, halves, tag, step_tag=None):
+            if step_tag:
+                step = activate(i, halves[0], step_tag)
+                total = slot(tag, [P, HALF], F32)
+                nc.vector.tensor_tensor(total[:], step[:], picked[i, halves[0]][:], ADD)
+            else:
+                sums = []
+                for h in halves:
+                    sums.append(add_turned(picked[i, 0][:, h * HALF : (h + 1) * HALF], activate(i, h, None)))
+                total = slot(tag, [P, J], F32)
+                for h in halves:
+                    turn_back(total[:, h * HALF : (h + 1) * HALF], sums[h])
+            totals[i, halves[0]] = total
+
+        def scatter(i, halves):
             page = pages[i % PAGES]
-            nc.vector.tensor_tensor(page[:].indirect(entries), total[:], gain[:, first : first + width], MULT)
+            weights = gain[:, halves[0] * HALF : (halves[-1] + 1) * HALF]
+            nc.vector.tensor_tensor(page[:].indirect(entries(halves)), totals[i, halves[0]][:], weights, MULT)
             if halves[-1] == HALVES - 1:
                 nc.sync.dma_start(out[i * P : (i + 1) * P, :], page[:])
 
         x_raw = {}
         un_raw = {}
-        x_raw[0] = load_rows(x, slice(0, HALF), ["R0", "R1"])
-        un_raw[0] = load_rows(un, slice(0, UN_CHUNK), ["V0", "V1"])
+        load_x(0, 0, "R0")
+        load_x(1, 0, "R1")
+        load_un(0, "V")
         wn_w = keep.tile([P, PASSES, 2 * N], U8, name="wn_w", align_bytes=64)
         nc.sync.dma_start(wn_w[:].bitcast(I32), wn_words.rearrange("a p b -> p a b").bitcast(I32))
         for q in range(4):
@@ -194,36 +220,53 @@ def tile_list_tgn_rnn_kernel(
         with nc.allow_non_contiguous_dma(reason="one bias value a partition"):
             nc.sync.dma_start(bias[:], bn.rearrange("(c p) -> p c", p=P))
         gain = keep.tile([P, J], F32, name="gain")
-        nc.sync.dma_start(gain[:, 0:HALF], wgo[:, 0:HALF])
+        nc.sync.dma_start(gain[:], wgo)
         load_h(1, "H1")
-        x_raw[1] = load_rows(x, slice(HALF, J), ["R2", "R3"])
-        un_raw[1] = load_rows(un, slice(UN_CHUNK, 2 * UN_CHUNK), ["V2", "V3"])
-        nc.sync.dma_start(gain[:, HALF:J], wgo[:, HALF:J])
-        load_h(2, "H2")
-        load_h(3, "H3")
 
         woven = un_weave(0, nc.vector.tensor_copy, "C")
         x_part(0, 0, "W", "X00")
         x_part(1, 0, "D", "X10")
         un_quant(0, woven, "U0")
-        un_raw[2] = load_rows(un, slice(2 * UN_CHUNK, 3 * UN_CHUNK), ["V0", "V1"])
-        load_h(4, "T")
-        un_raw[3] = load_rows(un, slice(3 * UN_CHUNK, 4 * UN_CHUNK), ["R0", "R1"])
-        unit(0, [0], "D", "B", "P1")
-        new_page(1)
-        unit(1, [0], "B", "F", "P2")
-        new_page(2)
-        x_part(0, 1, "D", "F")
-        x_part(1, 1, "B", "X11")
-        un_quant(1, un_weave(1, nc.scalar.copy, "R3"), "U1")
-        unit(0, [1], "C", "G", "W")
-        load_h(5, "H0")
-        unit(1, [1], "D", "H", "S")
-        load_h(6, "H1")
-        load_h(7, "R2")
-        unit(2, [0, 1], "B", "I")
-        un_quant(2, un_weave(2, nc.scalar.copy, "B"), "H")
-        unit(3, [0, 1], "R3", "J")
-        un_quant(3, un_weave(3, nc.scalar.copy, "R3"), "I")
-        for i in range(4, TILES):
-            unit(i, [0, 1], ["B", "R3"][i % 2], "JKL"[i % 3])
+        load_un(1, "V")
+        load_x(0, 1, "R0")
+        load_x(1, 1, "R1")
+        both = [0, 1]
+        gather(0, [0], "D")
+        gather(0, [1], "C")
+        combine(0, [0], "B", "P")
+        scatter(0, [0])
+        new_page(1, "P")
+        un_quant(1, un_weave(1, nc.scalar.copy, "D"), "U1")
+        gather(1, [0], "B")
+        combine(1, [0], "F", "E")
+        scatter(1, [0])
+        load_h(2, "H0")
+        load_un(2, "V")
+        x_part(0, 1, "B", "F")
+        load_h(3, "R0")
+        gather(1, [1], "D")
+        load_h(4, "H1")
+        x_part(1, 1, "E", "X11")
+        load_un(3, "R1")
+        gather(2, both, "E")
+        gather(3, both, "H0")
+        load_h(6, "R0")
+        combine(0, [1], "G", "S")
+        new_page(2, "S")
+        combine(1, [1], "H", "Z")
+        un_quant(2, un_weave(2, nc.scalar.copy, "B"), "U2")
+        load_h(5, "V")
+        un_quant(3, un_weave(3, nc.scalar.copy, "W"), "U3")
+        load_h(7, "R1")
+        scatter(0, [1])
+        scatter(1, [1])
+        tags = ["H0", "H", "E"]
+        combine(2, both, tags[2])
+        gather(4, both, tags[1])
+        combine(3, both, tags[0])
+        for i in range(2, TILES):
+            scatter(i, both)
+            if i + 3 < TILES:
+                gather(i + 3, both, tags[i % 3])
+            if i + 2 < TILES:
+                combine(i + 2, both, tags[(i + 2) % 3])

@@ -26,7 +26,7 @@ HALF = 512
 HALVES = J // HALF
 TILES = N // P
 UN_CHUNK = 256
-PAGES = 3
+PAGES = 2
 SPLIT_TILES = 2
 
 
@@ -46,16 +46,16 @@ def tile_list_tgn_rnn_kernel(
         offsets = lists.tile([P, J // 16], U16, name="offsets")
         nc.sync.dma_start(offsets[:], offs)
 
-        tab_s = slot("H0", [P, T], U8)
+        tab_s = slot("N", [P, T], U8)
         nc.sync.dma_start(tab_s[0:32, :].bitcast(I32), tab_scales.rearrange("a q t -> q a t").bitcast(I32))
         tab_w = slot("H1", [P, T], I32)
         nc.sync.dma_start(tab_w[:], tab_words[0].rearrange("p t b -> p (t b)").bitcast(I32))
+        wn_s = keep.tile([P, PASSES * N], U8, name="wn_s", align_bytes=64)
+        nc.vector.memset(wn_s[:].bitcast(I32), 0)
         nc.vector.memset(tab_s[32:64, :].bitcast(I32), 0)
         nc.vector.memset(tab_s[64:128, :].bitcast(I32), 0)
-        wn_s = keep.tile([P, PASSES, N], U8, name="wn_s", align_bytes=64)
-        v_s = keep.tile([P, PASSES, J], U8, name="v_s", align_bytes=64)
-        nc.vector.memset(wn_s[:].rearrange("p a n -> p (a n)").bitcast(I32), 0)
-        nc.vector.memset(v_s[:].rearrange("p a n -> p (a n)").bitcast(I32), 0)
+        v_s = keep.tile([P, PASSES * J], U8, name="v_s", align_bytes=64)
+        nc.vector.memset(v_s[:].bitcast(I32), 0)
         ident = keep.tile([P, P], F32, name="ident")
         make_identity(nc, ident[:])
 
@@ -63,18 +63,15 @@ def tile_list_tgn_rnn_kernel(
         nc.vector.tensor_copy(v_rows[:], tab_s[:].indirect(offsets[:]))
         for q in range(4):
             nc.sync.dma_start(
-                v_s[32 * q : 32 * q + 4, :, :].bitcast(I32), v_rows[8 * q : 8 * q + 8, :].bitcast(I32)
+                v_s[32 * q : 32 * q + 4, :].bitcast(I32), v_rows[8 * q : 8 * q + 8, :].bitcast(I32)
             )
-        pages = {0: keep.tile([P, T], F32, name="page0")}
-        nc.vector.memset(pages[0][:], 0.0)
+        pages = {b: keep.tile([P, T], F32, name="page%d" % b) for b in range(PAGES)}
+        for b in range(PAGES):
+            nc.vector.memset(pages[b][:], 0.0)
         v_pairs = slot("C", [P, J], U32)
         nc.vector.tensor_copy(v_pairs[:], tab_w[:].bitcast(U32).indirect(offsets[:]))
         v_words = keep.tile([P, PASSES, J], U16, name="v_words", align_bytes=64)
         nc.vector.tensor_copy(v_words[:], v_pairs[:].bitcast(U16).rearrange("p (j d) -> p d j", d=PASSES))
-
-        def new_page(b, tag):
-            pages[b] = slot(tag, [P, T], F32)
-            nc.gpsimd.memset(pages[b][:], 0.0)
 
         def load_rows(raw, src, a, cols):
             rows = src[a * K_PASS : (a + 1) * K_PASS, cols]
@@ -132,7 +129,7 @@ def tile_list_tgn_rnn_kernel(
                 nc.tensor.matmul_mx(
                     out=acc[:],
                     lhsT=wn_w[:, a, 2 * i * P : 2 * (i + 1) * P].bitcast(FP4X4),
-                    lhsT_scale=wn_s[:, a, i * P : (i + 1) * P],
+                    lhsT_scale=wn_s[:, a * N + i * P : a * N + (i + 1) * P],
                     rhs=x_q[a, h][0][:].bitcast(FP8X4),
                     rhs_scale=x_q[a, h][1][:],
                     start=(a == 0),
@@ -144,7 +141,7 @@ def tile_list_tgn_rnn_kernel(
                     lhsT=un_q[c][0][:, a * UN_CHUNK + off : a * UN_CHUNK + off + P].bitcast(FP8X4),
                     lhsT_scale=un_q[c][1][:, a * UN_CHUNK + off : a * UN_CHUNK + off + P],
                     rhs=v_words[:, a, cols].bitcast(FP4X4),
-                    rhs_scale=v_s[:, a, cols],
+                    rhs_scale=v_s[:, a * J + h * HALF : a * J + (h + 1) * HALF],
                     start=False,
                     stop=(a == PASSES - 1),
                 )
@@ -212,14 +209,14 @@ def tile_list_tgn_rnn_kernel(
         nc.sync.dma_start(wn_w[:].bitcast(I32), wn_words.rearrange("a p b -> p a b").bitcast(I32))
         for q in range(4):
             nc.gpsimd.dma_start(
-                wn_s[32 * q : 32 * q + 4, :, :].bitcast(I32),
+                wn_s[32 * q : 32 * q + 4, :].bitcast(I32),
                 wn_scales[:, 4 * q : 4 * q + 4, :].rearrange("a r n -> r a n").bitcast(I32),
             )
         load_h(0, "H0")
         bias = keep.tile([P, TILES], F32, name="bias")
         with nc.allow_non_contiguous_dma(reason="one bias value a partition"):
             nc.sync.dma_start(bias[:], bn.rearrange("(c p) -> p c", p=P))
-        gain = keep.tile([P, J], F32, name="gain")
+        gain = slot("N", [P, J], F32)
         nc.sync.dma_start(gain[:], wgo)
         load_h(1, "H1")
 
@@ -235,7 +232,6 @@ def tile_list_tgn_rnn_kernel(
         gather(0, [1], "C")
         combine(0, [0], "B", "P")
         scatter(0, [0])
-        new_page(1, "P")
         un_quant(1, un_weave(1, nc.scalar.copy, "D"), "U1")
         gather(1, [0], "B")
         combine(1, [0], "F", "E")
@@ -250,23 +246,23 @@ def tile_list_tgn_rnn_kernel(
         load_un(3, "R1")
         gather(2, both, "E")
         gather(3, both, "H0")
-        load_h(6, "R0")
         combine(0, [1], "G", "S")
-        new_page(2, "S")
         combine(1, [1], "H", "Z")
         un_quant(2, un_weave(2, nc.scalar.copy, "B"), "U2")
-        load_h(5, "V")
         un_quant(3, un_weave(3, nc.scalar.copy, "W"), "U3")
-        load_h(7, "R1")
         scatter(0, [1])
+        load_h(5, "G")
         scatter(1, [1])
         tags = ["H0", "H", "E"]
         combine(2, both, tags[2])
         gather(4, both, tags[1])
+        load_h(6, "H1")
         combine(3, both, tags[0])
         for i in range(2, TILES):
             scatter(i, both)
             if i + 3 < TILES:
                 gather(i + 3, both, tags[i % 3])
+            if i == 2:
+                load_h(7, "G")
             if i + 2 < TILES:
                 combine(i + 2, both, tags[(i + 2) % 3])

from contextlib import ExitStack

import concourse.mybir as mybir
from concourse.masks import make_identity

K, M, N, T, J = 1024, 1024, 1024, 2048, 1024
FLOPS = 2 * (K + M) * N * J

F32 = mybir.dt.float32
BF16 = mybir.dt.bfloat16
I32 = mybir.dt.int32
U32 = mybir.dt.uint32
U16 = mybir.dt.uint16
U8 = mybir.dt.uint8
FP8X4 = mybir.dt.float8_e4m3fn_x4
FP4X4 = mybir.dt.float4_e2m1fn_x4
MULT = mybir.AluOpType.mult
ADD = mybir.AluOpType.add
TANH = mybir.ActivationFunctionType.Tanh

P = 128
PACK = 4
K_PASS = P * PACK
PASSES = K // K_PASS
HALF = 512
HALVES = J // HALF
TILES = N // P
UN_CHUNK = 256
PAGES = 2
SPLIT_TILES = 2


def tile_list_tgn_rnn_kernel(
    tc, x, tab_words, tab_scales, wn_words, wn_scales, un, bn, hT, wgo, offs, out
):
    nc = tc.nc
    with ExitStack() as ctx:
        lists = ctx.enter_context(tc.tile_pool(name="lists", bufs=1))
        keep = ctx.enter_context(tc.tile_pool(name="keep", bufs=1))
        ring = ctx.enter_context(tc.tile_pool(name="ring", bufs=2))
        psum = ctx.enter_context(tc.psum_pool(name="psum", bufs=2))

        def slot(tag, shape, dtype):
            return keep.tile(shape, dtype, name="slot" + tag, tag="slot" + tag, align_bytes=64)

        offsets = lists.tile([P, J // 16], U16, name="offsets")
        nc.sync.dma_start(offsets[:], offs)

        tab_s = slot("N", [P, T], U8)
        nc.sync.dma_start(tab_s[0:32, :].bitcast(I32), tab_scales.rearrange("a q t -> q a t").bitcast(I32))
        tab_w = slot("H1", [P, T], I32)
        nc.sync.dma_start(tab_w[:], tab_words[0].rearrange("p t b -> p (t b)").bitcast(I32))
        wn_s = keep.tile([P, PASSES * N], U8, name="wn_s", align_bytes=64)
        nc.vector.memset(wn_s[:].bitcast(I32), 0)
        nc.vector.memset(tab_s[32:64, :].bitcast(I32), 0)
        nc.vector.memset(tab_s[64:128, :].bitcast(I32), 0)
        v_s = keep.tile([P, PASSES * J], U8, name="v_s", align_bytes=64)
        nc.vector.memset(v_s[:].bitcast(I32), 0)
        ident = keep.tile([P, P], F32, name="ident")
        make_identity(nc, ident[:])

        v_rows = keep.tile([P, J], U8, name="v_rows", align_bytes=64)
        nc.vector.tensor_copy(v_rows[:], tab_s[:].indirect(offsets[:]))
        for q in range(4):
            nc.sync.dma_start(
                v_s[32 * q : 32 * q + 4, :].bitcast(I32), v_rows[8 * q : 8 * q + 8, :].bitcast(I32)
            )
        pages = {b: keep.tile([P, T], F32, name="page%d" % b) for b in range(PAGES)}
        for b in range(PAGES):
            nc.vector.memset(pages[b][:], 0.0)
        v_pairs = slot("C", [P, J], U32)
        nc.vector.tensor_copy(v_pairs[:], tab_w[:].bitcast(U32).indirect(offsets[:]))
        v_words = keep.tile([P, PASSES, J], U16, name="v_words", align_bytes=64)
        nc.vector.tensor_copy(v_words[:], v_pairs[:].bitcast(U16).rearrange("p (j d) -> p d j", d=PASSES))

        def load_rows(raw, src, a, cols):
            rows = src[a * K_PASS : (a + 1) * K_PASS, cols]
            nc.sync.dma_start(raw, rows.rearrange("(p i) w -> p i w", i=PACK))

        def load_x(a, h, tag):
            raw = slot(tag, [P, PACK, HALF], F32)
            load_rows(raw[:], x, a, slice(h * HALF, (h + 1) * HALF))
            x_raw[a, h] = raw[:]

        def load_un(c, tag):
            raw = slot(tag, [P, PASSES * PACK * UN_CHUNK], F32)
            for a in range(PASSES):
                part = raw[:, a * PACK * UN_CHUNK : (a + 1) * PACK * UN_CHUNK].rearrange("p (i w) -> p i w", i=PACK)
                load_rows(part, un, a, slice(c * UN_CHUNK, (c + 1) * UN_CHUNK))
                un_raw[a, c] = part

        def weave(copy, woven, raw):
            copy(woven.rearrange("p (c u) i -> p c i u", u=4), raw.rearrange("p i (c u) -> p c i u", u=4))

        def quantise(woven, codes, label):
            scales = keep.tile([P, HALF], U8, name=label + "_scales", align_bytes=64)
            nc.vector.quantize_mx(
                out=codes[:].bitcast(FP8X4), scales=scales[:], in_=woven[:].rearrange("p w i -> p (w i)")
            )
            return codes, scales

        x_q = {}
        un_q = {}
        h_rows = {}

        def x_part(a, h, woven_tag, codes_tag):
            woven = slot(woven_tag, [P, HALF, PACK], BF16)
            weave(nc.scalar.copy, woven[:], x_raw[a, h])
            x_q[a, h] = quantise(woven, slot(codes_tag, [P, HALF], U32), "x%d%d" % (a, h))

        def un_weave(c, copy, woven_tag):
            woven = slot(woven_tag, [P, PASSES * UN_CHUNK, PACK], BF16)
            for a in range(PASSES):
                weave(copy, woven[:, a * UN_CHUNK : (a + 1) * UN_CHUNK, :], un_raw[a, c])
            return woven

        def un_quant(c, woven, codes_tag):
            un_q[c] = quantise(woven, slot(codes_tag, [P, PASSES * UN_CHUNK], U32), "un%d" % c)

        def load_h(i, tag):
            h_rows[i] = slot(tag, [P, T], F32)
            nc.sync.dma_start(h_rows[i][:], hT[i * P : (i + 1) * P, :])

        def activate(i, h, step_tag):
            acc = psum.tile([P, HALF], F32, name="acc", bufs=3)
            c, off = divmod(i * P, UN_CHUNK)
            cols = slice(h * HALF, (h + 1) * HALF)
            for a in range(PASSES):
                nc.tensor.matmul_mx(
                    out=acc[:],
                    lhsT=wn_w[:, a, 2 * i * P : 2 * (i + 1) * P].bitcast(FP4X4),
                    lhsT_scale=wn_s[:, a * N + i * P : a * N + (i + 1) * P],
                    rhs=x_q[a, h][0][:].bitcast(FP8X4),
                    rhs_scale=x_q[a, h][1][:],
                    start=(a == 0),
                    stop=False,
                )
            for a in range(PASSES):
                nc.tensor.matmul_mx(
                    out=acc[:],
                    lhsT=un_q[c][0][:, a * UN_CHUNK + off : a * UN_CHUNK + off + P].bitcast(FP8X4),
                    lhsT_scale=un_q[c][1][:, a * UN_CHUNK + off : a * UN_CHUNK + off + P],
                    rhs=v_words[:, a, cols].bitcast(FP4X4),
                    rhs_scale=v_s[:, a * J + h * HALF : a * J + (h + 1) * HALF],
                    start=False,
                    stop=(a == PASSES - 1),
                )
            if step_tag:
                step = slot(step_tag, [P, HALF], F32)
            else:
                step = ring.tile([P, HALF], F32, name="step", bufs=3)
            nc.scalar.activation(step[:], acc[:], TANH, bias=bias[:, i : i + 1])
            return step

        def add_turned(looked, step):
            turned = psum.tile([P, HALF], F32, name="turned", bufs=3)
            for b in range(HALF // P):
                blk = slice(b * P, (b + 1) * P)
                nc.tensor.matmul(turned[:, blk], looked[:, blk], ident[:], start=True, stop=False, is_transpose=True)
                nc.tensor.matmul(turned[:, blk], step[:, blk], ident[:], start=False, stop=True, is_transpose=True)
            turned_sb = ring.tile([P, HALF], F32, name="turned_sb", bufs=2)
            nc.scalar.copy(turned_sb[:], turned[:])
            return turned_sb

        def turn_back(total, turned_sb):
            back = psum.tile([P, HALF], F32, name="back", bufs=2)
            for b in range(HALF // P):
                blk = slice(b * P, (b + 1) * P)
                nc.tensor.transpose(back[:, blk], turned_sb[:, blk], ident[:])
            nc.scalar.copy(total, back[:])

        picked = {}
        totals = {}

        def entries(halves):
            return offsets[:, halves[0] * HALF // 16 : (halves[-1] + 1) * HALF // 16]

        def gather(i, halves, tag):
            picked[i, halves[0]] = slot(tag, [P, HALF * len(halves)], F32)
            nc.vector.tensor_copy(picked[i, halves[0]][:], h_rows[i][:].indirect(entries(halves)))

        def combine(i, halves, tag, step_tag=None):
            if step_tag:
                step = activate(i, halves[0], step_tag)
                total = slot(tag, [P, HALF], F32)
                nc.vector.tensor_tensor(total[:], step[:], picked[i, halves[0]][:], ADD)
            else:
                sums = []
                for h in halves:
                    sums.append(add_turned(picked[i, 0][:, h * HALF : (h + 1) * HALF], activate(i, h, None)))
                total = slot(tag, [P, J], F32)
                for h in halves:
                    turn_back(total[:, h * HALF : (h + 1) * HALF], sums[h])
            totals[i, halves[0]] = total

        def scatter(i, halves):
            page = pages[i % PAGES]
            weights = gain[:, halves[0] * HALF : (halves[-1] + 1) * HALF]
            nc.vector.tensor_tensor(page[:].indirect(entries(halves)), totals[i, halves[0]][:], weights, MULT)
            if halves[-1] == HALVES - 1:
                nc.sync.dma_start(out[i * P : (i + 1) * P, :], page[:])

        x_raw = {}
        un_raw = {}
        load_x(0, 0, "R0")
        load_x(1, 0, "R1")
        load_un(0, "V")
        wn_w = keep.tile([P, PASSES, 2 * N], U8, name="wn_w", align_bytes=64)
        nc.sync.dma_start(wn_w[:].bitcast(I32), wn_words.rearrange("a p b -> p a b").bitcast(I32))
        for q in range(4):
            nc.gpsimd.dma_start(
                wn_s[32 * q : 32 * q + 4, :].bitcast(I32),
                wn_scales[:, 4 * q : 4 * q + 4, :].rearrange("a r n -> r a n").bitcast(I32),
            )
        load_h(0, "H0")
        bias = keep.tile([P, TILES], F32, name="bias")
        with nc.allow_non_contiguous_dma(reason="one bias value a partition"):
            nc.sync.dma_start(bias[:], bn.rearrange("(c p) -> p c", p=P))
        gain = slot("N", [P, J], F32)
        nc.sync.dma_start(gain[:], wgo)
        load_h(1, "H1")

        woven = un_weave(0, nc.vector.tensor_copy, "C")
        x_part(0, 0, "W", "X00")
        x_part(1, 0, "D", "X10")
        un_quant(0, woven, "U0")
        load_un(1, "V")
        load_x(0, 1, "R0")
        load_x(1, 1, "R1")
        both = [0, 1]
        gather(0, [0], "D")
        gather(0, [1], "C")
        combine(0, [0], "B", "P")
        scatter(0, [0])
        un_quant(1, un_weave(1, nc.scalar.copy, "D"), "U1")
        gather(1, [0], "B")
        combine(1, [0], "F", "E")
        scatter(1, [0])
        load_h(2, "H0")
        load_un(2, "V")
        x_part(0, 1, "B", "F")
        load_h(3, "R0")
        gather(1, [1], "D")
        load_h(4, "H1")
        x_part(1, 1, "E", "X11")
        load_un(3, "R1")
        gather(2, both, "E")
        gather(3, both, "H0")
        combine(0, [1], "G", "S")
        combine(1, [1], "H", "Z")
        un_quant(2, un_weave(2, nc.scalar.copy, "B"), "U2")
        un_quant(3, un_weave(3, nc.scalar.copy, "W"), "U3")
        scatter(0, [1])
        load_h(5, "G")
        scatter(1, [1])
        tags = ["H0", "H", "E"]
        combine(2, both, tags[2])
        gather(4, both, tags[1])
        load_h(6, "H1")
        combine(3, both, tags[0])
        for i in range(2, TILES):
            scatter(i, both)
            if i + 3 < TILES:
                gather(i + 3, both, tags[i % 3])
            if i == 2:
                load_h(7, "G")
            if i + 2 < TILES:
                combine(i + 2, both, tags[(i + 2) % 3])
